import numpy as np
import ml_dtypes


def mxq(x, axis, fmt="e4m3"):
    dtype, down = {"e4m3": (ml_dtypes.float8_e4m3fn, 7), "e5m2": (ml_dtypes.float8_e5m2, 14)}[fmt]
    v = np.moveaxis(np.asarray(x, np.float32).astype(ml_dtypes.bfloat16).astype(np.float64), axis, -1)
    blocks = v.reshape(v.shape[:-1] + (-1, 32))
    amax = np.abs(blocks).max(-1, keepdims=True)
    byte = np.maximum(np.where(amax > 0, np.frexp(amax)[1] - 1 + 127, 0) - down, 1)
    scale = np.exp2(byte - 127.0)
    codes = (blocks / scale).astype(np.float32).astype(dtype).astype(np.float64)
    return np.moveaxis((codes * scale).reshape(v.shape), -1, axis)


WIDE = False


def mx_kscale(k):
    if not WIDE:
        return np.ones(k)
    levels = np.array([10, -10, 5, -5, 0])
    if k % 512:
        return np.exp2(np.random.permutation(np.resize(levels, k // 32))).repeat(32)
    a = np.empty((k // 512, 16))
    for p in range(k // 512):
        a[p, :8] = np.random.permutation(np.resize(levels, 8))
        for g in range(8):
            far = levels[np.abs(levels - a[p, g]) >= 10]
            a[p, g + 8] = far[np.random.randint(len(far))]
    return np.exp2(a.ravel()).repeat(32)


def f64(x):
    return np.asarray(x).astype(np.float64)


def striped(idx):
    return np.tile(idx.reshape(-1, 16).T, (8, 1)).astype(np.uint16)


def unstriped(offs):
    return offs[:16].T.reshape(-1).astype(np.int64)


E2M1 = np.array([0.0, 0.5, 1.0, 1.5, 2.0, 3.0, 4.0, 6.0, -0.0, -0.5, -1.0, -1.5, -2.0, -3.0, -4.0, -6.0])


def pack_weight(w, fmt):
    k, n = w.shape
    w = f64(np.asarray(w, np.float32).astype(ml_dtypes.bfloat16)).reshape(k // 32, 32, n)
    amax = np.abs(w).max(1)
    if fmt == "e4m3":
        byte = np.frexp(amax)[1] - 1 + 127 - 7
    else:
        mant, ex = np.frexp(amax / 6.0)
        byte = np.where(mant > 0.5, ex, ex - 1) + 127
    byte = np.clip(np.where(amax > 0, byte, 1), 1, 254)
    scaled = (w * np.exp2(127.0 - byte)[:, None, :]).reshape(k, n).astype(np.float32)
    by_word = np.ascontiguousarray(scaled.reshape(k // 512, 128, 4, n).transpose(0, 1, 3, 2))
    if fmt == "e4m3":
        words = by_word.astype(ml_dtypes.float8_e4m3fn).view(np.uint8)
    else:
        c = by_word.astype(ml_dtypes.float4_e2m1fn).view(np.uint8) & 0xF
        words = (c[..., 0::2] | (c[..., 1::2] << 4)).reshape(k // 512, 128, 2 * n)
    return np.ascontiguousarray(words), np.ascontiguousarray(byte.astype(np.uint8).reshape(k // 512, 16, n))


def unpack_weight(words, scales, fmt):
    g, _, n = scales.shape
    words = np.ascontiguousarray(words).reshape(g, 128, n, -1)
    if fmt == "e4m3":
        vals = words.view(ml_dtypes.float8_e4m3fn).astype(np.float64)
    else:
        nib = np.empty((g, 128, n, 4), np.uint8)
        nib[..., 0::2] = words & 0xF
        nib[..., 1::2] = words >> 4
        vals = E2M1[nib]
    vals = vals * np.repeat(np.exp2(scales.astype(np.float64) - 127.0), 8, axis=1)[..., None]
    return vals.transpose(0, 1, 3, 2).reshape(g * 512, n)


def silu(v):
    return v / (1.0 + np.exp(-np.maximum(v, -700.0)))


K, T, E, C, N = 1024, 768, 6, 256, 128


def by_expert(wq, xq):
    return np.concatenate([wq[e].T @ xq[:, e * C:(e + 1) * C] for e in range(E)], axis=1)


def setup_inputs():
    n = np.random.standard_normal
    s = mx_kscale(K)[:, None]
    first = np.random.permutation(np.repeat(np.arange(E), T // E))
    second = (first + 1 + np.random.permutation(np.repeat(np.arange(E - 1), -(-T // (E - 1)))[:T])) % E
    while np.bincount(second, minlength=E).max() != T // E:
        load = np.bincount(second, minlength=E); hi, lo = int(load.argmax()), int(load.argmin())
        t = np.flatnonzero((second == hi) & (first != lo))[0]; second[t] = lo
    slot_token = np.empty(E * C, np.int64); pos = np.empty((2, T), np.int64); fill = np.zeros(E, np.int64)
    place = np.stack([np.random.permutation(C) for _ in range(E)])
    for r, deal in enumerate((first, second)):
        for t in np.random.permutation(T):
            e = deal[t]; j = e * C + place[e, fill[e]]; fill[e] += 1; slot_token[j] = t; pos[r, t] = j
    g = np.random.uniform(0.2, 0.8, T)
    w = [pack_weight(m, "e2m1") for m in n((E, K, N)) / np.sqrt(K) / s[None]]
    w_slot = np.empty(E * C); w_slot[pos[0]] = g; w_slot[pos[1]] = 1.0 - g
    return {
        "xT": (n((K, T)) * s).astype(np.float32),
        "w_words": np.stack([m[0] for m in w]),
        "w_scales": np.stack([m[1] for m in w]),
        "b": (0.3 * n((N, E))).astype(np.float32),
        "gate": np.tile(w_slot, (K, 1)).astype(np.float32),
        "offs": striped(slot_token),
        "pos1": striped(pos[0]),
        "pos2": striped(pos[1]),
    }


def reference(xT, w_words, w_scales, b, gate, offs, pos1, pos2):
    idx = unstriped(offs)
    w = np.stack([unpack_weight(w_words[e], w_scales[e], "e2m1") for e in range(E)])
    xq = mxq(f64(gate) * f64(xT)[:, idx], 0, "e4m3")
    y = by_expert(w, xq)
    y = silu(y + np.repeat(f64(b), C, axis=1))
    return y[:, unstriped(pos1)] + y[:, unstriped(pos2)]

@@ -1,0 +1,130 @@
+from contextlib import ExitStack
+
+import concourse.mybir as mybir
+
+K, T, E, C, N = 1024, 768, 6, 256, 128
+S = E * C
+FLOPS = 2 * K * N * S
+BYTES = 4 * K * T + E * K * N // 2 + E * K * N // 32 + 4 * N * E + 4 * S + 2 * 128 * (S + 2 * T) // 16 + 4 * N * T
+
+F32 = mybir.dt.float32
+BF16 = mybir.dt.bfloat16
+I32 = mybir.dt.int32
+U32 = mybir.dt.uint32
+U16 = mybir.dt.uint16
+U8 = mybir.dt.uint8
+FP8X4 = mybir.dt.float8_e4m3fn_x4
+FP4X4 = mybir.dt.float4_e2m1fn_x4
+MULT = mybir.AluOpType.mult
+ADD = mybir.AluOpType.add
+SILU = mybir.ActivationFunctionType.Silu
+
+P = 128
+PACK = 4
+PASSES = K // (P * PACK)
+MOVE = 128
+GATE = 512
+UNITS = [(0, 0, 512), (1, 0, 512), (0, 512, 512), (1, 512, 512), (0, 1024, 512), (1, 1024, 256), (1, 1280, 128), (1, 1408, 128)]
+PARTS = [512, 256]
+
+
+def tile_moe_pre_lin_silu_kernel(tc, xT, w_words, w_scales, b, gate, offs, pos1, pos2, out):
+    nc = tc.nc
+    with ExitStack() as ctx:
+        keep = ctx.enter_context(tc.tile_pool(name="keep", bufs=1))
+        ring = ctx.enter_context(tc.tile_pool(name="ring", bufs=2))
+        psum = ctx.enter_context(tc.psum_pool(name="psum", bufs=4))
+
+        offs_t = keep.tile([P, S // 16], U16, name="offs_t")
+        pos1_t = keep.tile([P, T // 16], U16, name="pos1_t")
+        pos2_t = keep.tile([P, T // 16], U16, name="pos2_t")
+        w_sc = keep.tile([P, E * PASSES * N], U8, name="w_sc", align_bytes=64)
+        nc.gpsimd.memset(w_sc[:].bitcast(I32), 0)
+
+        x_rows = xT.rearrange("(a p j) t -> a j p t", a=PASSES, j=PACK)
+        planes = [[keep.tile([P, T], F32, name="x%d_%d" % (a, j)) for j in range(PACK)] for a in range(PASSES)]
+        gates = [keep.tile([P, GATE], F32, name="gate%d" % c) for c in range(S // GATE)]
+
+        nc.sync.dma_start(planes[0][0][:], x_rows[0, 0])
+        nc.sync.dma_start(offs_t[:], offs)
+        nc.sync.dma_start(gates[0][:], gate[0:P, 0:GATE])
+        for a in range(PASSES):
+            for j in range(PACK):
+                if a + j > 0:
+                    nc.sync.dma_start(planes[a][j][:], x_rows[a, j])
+        for c in range(1, S // GATE):
+            nc.sync.dma_start(gates[c][:], gate[0:P, c * GATE:(c + 1) * GATE])
+        w_t = keep.tile([P, E * PASSES, 2 * N], U8, name="w_t", align_bytes=64)
+        nc.sync.dma_start(w_t[:].bitcast(I32), w_words.rearrange("e a p b -> p (e a) b").bitcast(I32))
+        sc_rows = w_scales.rearrange("e a (q r) n -> r q (e a) n", r=4)
+        sc_view = w_sc[:].rearrange("p (g n) -> p g n", n=N)
+        for r in range(4):
+            nc.sync.dma_start(sc_view[r:P:32].bitcast(I32), sc_rows[r].bitcast(I32))
+        b_t = keep.tile([P, E], F32, name="b_t")
+        nc.sync.dma_start(b_t[:], b)
+        nc.sync.dma_start(pos1_t[:], pos1)
+        nc.sync.dma_start(pos2_t[:], pos2)
+
+        y = keep.tile([P, S], F32, name="y")
+        made = {}
+
+        def gather(a, s0, n):
+            g4 = ring.tile([P, PACK, n], F32, name="g4")
+            lst = offs_t[:, s0 // 16:(s0 + n) // 16]
+            weight = gates[s0 // GATE][:, s0 % GATE:s0 % GATE + n]
+            for j in range(PACK):
+                nc.vector.tensor_tensor(g4[:, j, :], planes[a][j][:].indirect(lst), weight, MULT)
+            xb = ring.tile([P, n, PACK], BF16, name="xb", align_bytes=64)
+            nc.scalar.copy(
+                xb[:].rearrange("p (c i) t -> p c t i", i=4),
+                g4[:].rearrange("p t (c i) -> p c t i", i=4),
+            )
+            return xb
+
+        def quantize(a, s0, n, xb):
+            codes = keep.tile([P, n], U32, name="codes%d_%d" % (a, s0), align_bytes=64)
+            scales = keep.tile([P, n], U8, name="scales%d_%d" % (a, s0), align_bytes=64)
+            nc.vector.quantize_mx(out=codes[:].bitcast(FP8X4), scales=scales[:], in_=xb[:].rearrange("p n t -> p (n t)"))
+            for h in range(0, n, MOVE):
+                made[a, s0 + h] = (codes[:, h:h + MOVE], scales[:, h:h + MOVE])
+
+        def multiply(s0, n):
+            acc = psum.tile([P, n], F32, name="acc")
+            for h in range(0, n, MOVE):
+                e = (s0 + h) // C
+                for a in range(PASSES):
+                    g = e * PASSES + a
+                    codes, scales = made[a, s0 + h]
+                    nc.tensor.matmul_mx(
+                        out=acc[:, h:h + MOVE],
+                        lhsT=w_t[:, g, :].bitcast(FP4X4),
+                        lhsT_scale=w_sc[:, g * N:(g + 1) * N],
+                        rhs=codes.bitcast(FP8X4),
+                        rhs_scale=scales,
+                        start=(a == 0), stop=(a == PASSES - 1))
+            m = min(n, C)
+            for h in range(0, n, m):
+                e = (s0 + h) // C
+                nc.scalar.activation(y[:, s0 + h:s0 + h + m], acc[:, h:h + m], SILU, bias=b_t[:, e:e + 1])
+
+        def finish(a, s0, n, xb):
+            quantize(a, s0, n, xb)
+            if a == PASSES - 1:
+                multiply(s0, n)
+
+        pending = []
+        for a, s0, n in UNITS:
+            xb = gather(a, s0, n)
+            for item in pending:
+                finish(*item)
+            pending = [(a, s0, n, xb)]
+        finish(*pending[0])
+
+        begins = [sum(PARTS[:i]) for i in range(len(PARTS))]
+        firsts = [keep.tile([P, n], F32, name="first%d" % i) for i, n in enumerate(PARTS)]
+        for i, n in enumerate(PARTS):
+            nc.vector.tensor_copy(firsts[i][:], y[:].indirect(pos1_t[:, begins[i] // 16:(begins[i] + n) // 16]))
+        for i, n in enumerate(PARTS):
+            both = keep.tile([P, n], F32, name="both%d" % i)
+            nc.vector.tensor_tensor(both[:], y[:].indirect(pos2_t[:, begins[i] // 16:(begins[i] + n) // 16]), firsts[i][:], ADD)
+            nc.sync.dma_start(out[:, begins[i]:begins[i] + n], both[:])

@@ -23,8 +23,11 @@ P = 128
 PACK = 4
 PASSES = K // (P * PACK)
 MOVE = 128
-GATE = 512
-UNITS = [(0, 0, 512), (1, 0, 512), (0, 512, 512), (1, 512, 512), (0, 1024, 512), (1, 1024, 256), (1, 1280, 128), (1, 1408, 128)]
+GATE = [128, 256, 640, 512]
+UNITS = [(0, 0, 1024), (1, 0, 1024), (0, 1024, 512), (1, 1024, 384), (1, 1408, 128)]
+PIECES = [[512, 512], [512, 512], [512], [256, 128], [128]]
+REUSE = {2: (0, 1), 3: (1, 1), 4: (2, 0)}
+SPARE = 16
 PARTS = [512, 256]
 
 
@@ -32,8 +35,7 @@ def tile_moe_pre_lin_silu_kernel(tc, xT, w_words, w_scales, b, gate, offs, pos1,
     nc = tc.nc
     with ExitStack() as ctx:
         keep = ctx.enter_context(tc.tile_pool(name="keep", bufs=1))
-        ring = ctx.enter_context(tc.tile_pool(name="ring", bufs=2))
-        psum = ctx.enter_context(tc.psum_pool(name="psum", bufs=4))
+        psum = ctx.enter_context(tc.psum_pool(name="psum", bufs=6))
 
         offs_t = keep.tile([P, S // 16], U16, name="offs_t")
         pos1_t = keep.tile([P, T // 16], U16, name="pos1_t")
@@ -42,18 +44,24 @@ def tile_moe_pre_lin_silu_kernel(tc, xT, w_words, w_scales, b, gate, offs, pos1,
         nc.gpsimd.memset(w_sc[:].bitcast(I32), 0)
 
         x_rows = xT.rearrange("(a p j) t -> a j p t", a=PASSES, j=PACK)
-        planes = [[keep.tile([P, T], F32, name="x%d_%d" % (a, j)) for j in range(PACK)] for a in range(PASSES)]
-        gates = [keep.tile([P, GATE], F32, name="gate%d" % c) for c in range(S // GATE)]
+        widths = [max([T] + [n for ua, s0, n in UNITS if ua == a]) + SPARE for a in range(PASSES)]
+        planes = [[keep.tile([P, widths[a]], F32, name="x%d_%d" % (a, j)) for j in range(PACK)] for a in range(PASSES)]
+        for a in range(PASSES):
+            for j in range(PACK):
+                (nc.vector if a == 0 else nc.gpsimd).memset(planes[a][j][:, T:], 0.0)
+        gate_t = keep.tile([P, S], F32, name="gate_t")
+        gate_cuts = [(sum(GATE[:c]), n) for c, n in enumerate(GATE)]
 
-        nc.sync.dma_start(planes[0][0][:], x_rows[0, 0])
+        nc.sync.dma_start(planes[0][0][:, :T], x_rows[0, 0])
         nc.sync.dma_start(offs_t[:], offs)
-        nc.sync.dma_start(gates[0][:], gate[0:P, 0:GATE])
+        for s0, n in gate_cuts[:3]:
+            nc.sync.dma_start(gate_t[:, s0:s0 + n], gate[0:P, s0:s0 + n])
         for a in range(PASSES):
             for j in range(PACK):
                 if a + j > 0:
-                    nc.sync.dma_start(planes[a][j][:], x_rows[a, j])
-        for c in range(1, S // GATE):
-            nc.sync.dma_start(gates[c][:], gate[0:P, c * GATE:(c + 1) * GATE])
+                    nc.sync.dma_start(planes[a][j][:, :T], x_rows[a, j])
+        for s0, n in gate_cuts[3:]:
+            nc.sync.dma_start(gate_t[:, s0:s0 + n], gate[0:P, s0:s0 + n])
         w_t = keep.tile([P, E * PASSES, 2 * N], U8, name="w_t", align_bytes=64)
         nc.sync.dma_start(w_t[:].bitcast(I32), w_words.rearrange("e a p b -> p (e a) b").bitcast(I32))
         sc_rows = w_scales.rearrange("e a (q r) n -> r q (e a) n", r=4)
@@ -68,18 +76,25 @@ def tile_moe_pre_lin_silu_kernel(tc, xT, w_words, w_scales, b, gate, offs, pos1,
         y = keep.tile([P, S], F32, name="y")
         made = {}
 
-        def gather(a, s0, n):
-            g4 = ring.tile([P, PACK, n], F32, name="g4")
-            lst = offs_t[:, s0 // 16:(s0 + n) // 16]
-            weight = gates[s0 // GATE][:, s0 % GATE:s0 % GATE + n]
+        def gather(u):
+            a, s0, n = UNITS[u]
+            tag = "xb%d_%d" % REUSE[u] if u in REUSE else "g%d" % u
+            g4 = keep.tile([P, PACK, n], F32, name="g4_%d" % u, tag=tag, align_bytes=64)
             for j in range(PACK):
-                nc.vector.tensor_tensor(g4[:, j, :], planes[a][j][:].indirect(lst), weight, MULT)
-            xb = ring.tile([P, n, PACK], BF16, name="xb", align_bytes=64)
-            nc.scalar.copy(
-                xb[:].rearrange("p (c i) t -> p c t i", i=4),
-                g4[:].rearrange("p t (c i) -> p c t i", i=4),
-            )
-            return xb
+                for c0, m in (gate_cuts[:3] if u + j == 0 else [(s0, n)]):
+                    lst = offs_t[:, c0 // 16:(c0 + m) // 16]
+                    nc.vector.tensor_tensor(g4[:, j, c0 - s0:c0 - s0 + m], planes[a][j][:].indirect(lst), gate_t[:, c0:c0 + m], MULT)
+            pieces = []
+            h = 0
+            for i, m in enumerate(PIECES[u]):
+                xb = keep.tile([P, m, PACK], BF16, name="xb_%d_%d" % (u, i), tag="xb%d_%d" % (u, i), align_bytes=64)
+                nc.scalar.copy(
+                    xb[:].rearrange("p (c i) t -> p c t i", i=4),
+                    g4[:, :, h:h + m].rearrange("p t (c i) -> p c t i", i=4),
+                )
+                pieces.append((a, s0 + h, m, xb))
+                h = h + m
+            return pieces
 
         def quantize(a, s0, n, xb):
             codes = keep.tile([P, n], U32, name="codes%d_%d" % (a, s0), align_bytes=64)
@@ -88,37 +103,34 @@ def tile_moe_pre_lin_silu_kernel(tc, xT, w_words, w_scales, b, gate, offs, pos1,
             for h in range(0, n, MOVE):
                 made[a, s0 + h] = (codes[:, h:h + MOVE], scales[:, h:h + MOVE])
 
+        accs = {}
+
         def multiply(s0, n):
-            acc = psum.tile([P, n], F32, name="acc")
-            for h in range(0, n, MOVE):
-                e = (s0 + h) // C
+            for h in range(s0, s0 + n, MOVE):
+                e = h // C
+                if h % C == 0:
+                    accs[e] = psum.tile([P, C], F32, name="acc")
                 for a in range(PASSES):
                     g = e * PASSES + a
-                    codes, scales = made[a, s0 + h]
+                    codes, scales = made[a, h]
                     nc.tensor.matmul_mx(
-                        out=acc[:, h:h + MOVE],
+                        out=accs[e][:, h % C:h % C + MOVE],
                         lhsT=w_t[:, g, :].bitcast(FP4X4),
                         lhsT_scale=w_sc[:, g * N:(g + 1) * N],
                         rhs=codes.bitcast(FP8X4),
                         rhs_scale=scales,
                         start=(a == 0), stop=(a == PASSES - 1))
-            m = min(n, C)
-            for h in range(0, n, m):
-                e = (s0 + h) // C
-                nc.scalar.activation(y[:, s0 + h:s0 + h + m], acc[:, h:h + m], SILU, bias=b_t[:, e:e + 1])
+                if (h + MOVE) % C == 0:
+                    nc.scalar.activation(y[:, e * C:(e + 1) * C], accs[e][:], SILU, bias=b_t[:, e:e + 1])
 
         def finish(a, s0, n, xb):
             quantize(a, s0, n, xb)
             if a == PASSES - 1:
                 multiply(s0, n)
 
-        pending = []
-        for a, s0, n in UNITS:
-            xb = gather(a, s0, n)
-            for item in pending:
+        for u in range(len(UNITS)):
+            for item in gather(u):
                 finish(*item)
-            pending = [(a, s0, n, xb)]
-        finish(*pending[0])
 
         begins = [sum(PARTS[:i]) for i in range(len(PARTS))]
         firsts = [keep.tile([P, n], F32, name="first%d" % i) for i, n in enumerate(PARTS)]

@@ -41,14 +41,18 @@ def tile_moe_pre_lin_silu_kernel(tc, xT, w_words, w_scales, b, gate, offs, pos1,
         pos1_t = keep.tile([P, T // 16], U16, name="pos1_t")
         pos2_t = keep.tile([P, T // 16], U16, name="pos2_t")
         w_sc = keep.tile([P, E * PASSES * N], U8, name="w_sc", align_bytes=64)
-        nc.gpsimd.memset(w_sc[:].bitcast(I32), 0)
+        nc.vector.memset(w_sc[:].bitcast(I32), 0)
+
+        warm = keep.tile([P, 2], F32, name="warm")
+        nc.vector.memset(warm[:, 0:1], 0.0)
+        nc.scalar.activation(warm[:, 1:2], warm[:, 0:1], SILU)
 
         x_rows = xT.rearrange("(a p j) t -> a j p t", a=PASSES, j=PACK)
         widths = [max([T] + [n for ua, s0, n in UNITS if ua == a]) + SPARE for a in range(PASSES)]
         planes = [[keep.tile([P, widths[a]], F32, name="x%d_%d" % (a, j)) for j in range(PACK)] for a in range(PASSES)]
         for a in range(PASSES):
             for j in range(PACK):
-                (nc.vector if a == 0 else nc.gpsimd).memset(planes[a][j][:, T:], 0.0)
+                nc.vector.memset(planes[a][j][:, T:], 0.0)
         gate_t = keep.tile([P, S], F32, name="gate_t")
         gate_cuts = [(sum(GATE[:c]), n) for c, n in enumerate(GATE)]
 

from contextlib import ExitStack

import concourse.mybir as mybir

K, T, E, C, N = 1024, 768, 6, 256, 128
S = E * C
FLOPS = 2 * K * N * S
BYTES = 4 * K * T + E * K * N // 2 + E * K * N // 32 + 4 * N * E + 4 * S + 2 * 128 * (S + 2 * T) // 16 + 4 * N * T

F32 = mybir.dt.float32
BF16 = mybir.dt.bfloat16
I32 = mybir.dt.int32
U32 = mybir.dt.uint32
U16 = mybir.dt.uint16
U8 = mybir.dt.uint8
FP8X4 = mybir.dt.float8_e4m3fn_x4
FP4X4 = mybir.dt.float4_e2m1fn_x4
MULT = mybir.AluOpType.mult
ADD = mybir.AluOpType.add
SILU = mybir.ActivationFunctionType.Silu

P = 128
PACK = 4
PASSES = K // (P * PACK)
MOVE = 128
GATE = [128, 256, 640, 512]
UNITS = [(0, 0, 1024), (1, 0, 1024), (0, 1024, 512), (1, 1024, 384), (1, 1408, 128)]
PIECES = [[512, 512], [512, 512], [512], [256, 128], [128]]
REUSE = {2: (0, 1), 3: (1, 1), 4: (2, 0)}
SPARE = 16
PARTS = [512, 256]


def tile_moe_pre_lin_silu_kernel(tc, xT, w_words, w_scales, b, gate, offs, pos1, pos2, out):
    nc = tc.nc
    with ExitStack() as ctx:
        keep = ctx.enter_context(tc.tile_pool(name="keep", bufs=1))
        psum = ctx.enter_context(tc.psum_pool(name="psum", bufs=6))

        offs_t = keep.tile([P, S // 16], U16, name="offs_t")
        pos1_t = keep.tile([P, T // 16], U16, name="pos1_t")
        pos2_t = keep.tile([P, T // 16], U16, name="pos2_t")
        w_sc = keep.tile([P, E * PASSES * N], U8, name="w_sc", align_bytes=64)
        nc.vector.memset(w_sc[:].bitcast(I32), 0)

        warm = keep.tile([P, 2], F32, name="warm")
        nc.vector.memset(warm[:, 0:1], 0.0)
        nc.scalar.activation(warm[:, 1:2], warm[:, 0:1], SILU)

        x_rows = xT.rearrange("(a p j) t -> a j p t", a=PASSES, j=PACK)
        widths = [max([T] + [n for ua, s0, n in UNITS if ua == a]) + SPARE for a in range(PASSES)]
        planes = [[keep.tile([P, widths[a]], F32, name="x%d_%d" % (a, j)) for j in range(PACK)] for a in range(PASSES)]
        for a in range(PASSES):
            for j in range(PACK):
                nc.vector.memset(planes[a][j][:, T:], 0.0)
        gate_t = keep.tile([P, S], F32, name="gate_t")
        gate_cuts = [(sum(GATE[:c]), n) for c, n in enumerate(GATE)]

        nc.sync.dma_start(planes[0][0][:, :T], x_rows[0, 0])
        nc.sync.dma_start(offs_t[:], offs)
        for s0, n in gate_cuts[:3]:
            nc.sync.dma_start(gate_t[:, s0:s0 + n], gate[0:P, s0:s0 + n])
        for a in range(PASSES):
            for j in range(PACK):
                if a + j > 0:
                    nc.sync.dma_start(planes[a][j][:, :T], x_rows[a, j])
        for s0, n in gate_cuts[3:]:
            nc.sync.dma_start(gate_t[:, s0:s0 + n], gate[0:P, s0:s0 + n])
        w_t = keep.tile([P, E * PASSES, 2 * N], U8, name="w_t", align_bytes=64)
        nc.sync.dma_start(w_t[:].bitcast(I32), w_words.rearrange("e a p b -> p (e a) b").bitcast(I32))
        sc_rows = w_scales.rearrange("e a (q r) n -> r q (e a) n", r=4)
        sc_view = w_sc[:].rearrange("p (g n) -> p g n", n=N)
        for r in range(4):
            nc.sync.dma_start(sc_view[r:P:32].bitcast(I32), sc_rows[r].bitcast(I32))
        b_t = keep.tile([P, E], F32, name="b_t")
        nc.sync.dma_start(b_t[:], b)
        nc.sync.dma_start(pos1_t[:], pos1)
        nc.sync.dma_start(pos2_t[:], pos2)

        y = keep.tile([P, S], F32, name="y")
        made = {}

        def gather(u):
            a, s0, n = UNITS[u]
            tag = "xb%d_%d" % REUSE[u] if u in REUSE else "g%d" % u
            g4 = keep.tile([P, PACK, n], F32, name="g4_%d" % u, tag=tag, align_bytes=64)
            for j in range(PACK):
                for c0, m in (gate_cuts[:3] if u + j == 0 else [(s0, n)]):
                    lst = offs_t[:, c0 // 16:(c0 + m) // 16]
                    nc.vector.tensor_tensor(g4[:, j, c0 - s0:c0 - s0 + m], planes[a][j][:].indirect(lst), gate_t[:, c0:c0 + m], MULT)
            pieces = []
            h = 0
            for i, m in enumerate(PIECES[u]):
                xb = keep.tile([P, m, PACK], BF16, name="xb_%d_%d" % (u, i), tag="xb%d_%d" % (u, i), align_bytes=64)
                nc.scalar.copy(
                    xb[:].rearrange("p (c i) t -> p c t i", i=4),
                    g4[:, :, h:h + m].rearrange("p t (c i) -> p c t i", i=4),
                )
                pieces.append((a, s0 + h, m, xb))
                h = h + m
            return pieces

        def quantize(a, s0, n, xb):
            codes = keep.tile([P, n], U32, name="codes%d_%d" % (a, s0), align_bytes=64)
            scales = keep.tile([P, n], U8, name="scales%d_%d" % (a, s0), align_bytes=64)
            nc.vector.quantize_mx(out=codes[:].bitcast(FP8X4), scales=scales[:], in_=xb[:].rearrange("p n t -> p (n t)"))
            for h in range(0, n, MOVE):
                made[a, s0 + h] = (codes[:, h:h + MOVE], scales[:, h:h + MOVE])

        accs = {}

        def multiply(s0, n):
            for h in range(s0, s0 + n, MOVE):
                e = h // C
                if h % C == 0:
                    accs[e] = psum.tile([P, C], F32, name="acc")
                for a in range(PASSES):
                    g = e * PASSES + a
                    codes, scales = made[a, h]
                    nc.tensor.matmul_mx(
                        out=accs[e][:, h % C:h % C + MOVE],
                        lhsT=w_t[:, g, :].bitcast(FP4X4),
                        lhsT_scale=w_sc[:, g * N:(g + 1) * N],
                        rhs=codes.bitcast(FP8X4),
                        rhs_scale=scales,
                        start=(a == 0), stop=(a == PASSES - 1))
                if (h + MOVE) % C == 0:
                    nc.scalar.activation(y[:, e * C:(e + 1) * C], accs[e][:], SILU, bias=b_t[:, e:e + 1])

        def finish(a, s0, n, xb):
            quantize(a, s0, n, xb)
            if a == PASSES - 1:
                multiply(s0, n)

        for u in range(len(UNITS)):
            for item in gather(u):
                finish(*item)

        begins = [sum(PARTS[:i]) for i in range(len(PARTS))]
        firsts = [keep.tile([P, n], F32, name="first%d" % i) for i, n in enumerate(PARTS)]
        for i, n in enumerate(PARTS):
            nc.vector.tensor_copy(firsts[i][:], y[:].indirect(pos1_t[:, begins[i] // 16:(begins[i] + n) // 16]))
        for i, n in enumerate(PARTS):
            both = keep.tile([P, n], F32, name="both%d" % i)
            nc.vector.tensor_tensor(both[:], y[:].indirect(pos2_t[:, begins[i] // 16:(begins[i] + n) // 16]), firsts[i][:], ADD)
            nc.sync.dma_start(out[:, begins[i]:begins[i] + n], both[:])
